import numpy as np
import ml_dtypes


def mxq(x, axis, fmt="e4m3"):
    dtype, down = {"e4m3": (ml_dtypes.float8_e4m3fn, 7), "e5m2": (ml_dtypes.float8_e5m2, 14)}[fmt]
    v = np.moveaxis(np.asarray(x, np.float32).astype(ml_dtypes.bfloat16).astype(np.float64), axis, -1)
    blocks = v.reshape(v.shape[:-1] + (-1, 32))
    amax = np.abs(blocks).max(-1, keepdims=True)
    byte = np.maximum(np.where(amax > 0, np.frexp(amax)[1] - 1 + 127, 0) - down, 1)
    scale = np.exp2(byte - 127.0)
    codes = (blocks / scale).astype(np.float32).astype(dtype).astype(np.float64)
    return np.moveaxis((codes * scale).reshape(v.shape), -1, axis)


WIDE = False


def mx_kscale(k):
    if not WIDE:
        return np.ones(k)
    levels = np.array([10, -10, 5, -5, 0])
    if k % 512:
        return np.exp2(np.random.permutation(np.resize(levels, k // 32))).repeat(32)
    a = np.empty((k // 512, 16))
    for p in range(k // 512):
        a[p, :8] = np.random.permutation(np.resize(levels, 8))
        for g in range(8):
            far = levels[np.abs(levels - a[p, g]) >= 10]
            a[p, g + 8] = far[np.random.randint(len(far))]
    return np.exp2(a.ravel()).repeat(32)


def f64(x):
    return np.asarray(x).astype(np.float64)


def striped(idx):
    return np.tile(idx.reshape(-1, 16).T, (8, 1)).astype(np.uint16)


def unstriped(offs):
    return offs[:16].T.reshape(-1).astype(np.int64)


def pack_weight(w):
    k, n = w.shape
    w = f64(np.asarray(w, np.float32).astype(ml_dtypes.bfloat16)).reshape(k // 32, 32, n)
    amax = np.abs(w).max(1)
    byte = np.clip(np.where(amax > 0, np.frexp(amax)[1] - 1 + 127 - 7, 1), 1, 254)
    scaled = (w * np.exp2(127.0 - byte)[:, None, :]).reshape(k, n).astype(np.float32)
    words = np.ascontiguousarray(scaled.reshape(k // 512, 128, 4, n).transpose(0, 1, 3, 2)).astype(ml_dtypes.float8_e4m3fn).view(np.uint8)
    return words, np.ascontiguousarray(byte.astype(np.uint8).reshape(k // 512, 16, n))


def unpack_weight(words, scales):
    g, p, n, _ = words.shape
    vals = np.ascontiguousarray(words).view(ml_dtypes.float8_e4m3fn).astype(np.float64) * np.repeat(np.exp2(scales.astype(np.float64) - 127.0), 8, axis=1)[..., None]
    return vals.transpose(0, 1, 3, 2).reshape(g * 512, n)


def relu(v):
    return np.maximum(v, 0.0)

def planes(y):
    n, m = y.shape
    v = y.astype(np.float32).astype(ml_dtypes.bfloat16).astype(np.float64).reshape(n // 32, 32, m)
    top = np.abs(v).max(1)
    byte = np.clip(np.where(top > 0, np.frexp(top)[1] - 1 + 127 - 7, 1), 1, 254)
    codes = (v * np.exp2(127.0 - byte)[:, None, :]).reshape(n, m).astype(np.float32).astype(ml_dtypes.float8_e4m3fn).view(np.uint8)
    words = codes.reshape(n // 512, 128, 4, m).transpose(0, 1, 3, 2)
    return np.ascontiguousarray(words), np.ascontiguousarray(byte.astype(np.uint8).reshape(n // 512, 16, m))


K, T, S, V, N = 512, 1024, 512, 256, 512


def setup_inputs():
    n = np.random.standard_normal
    s = mx_kscale(K)[:, None]
    packed_xT = pack_weight(n((K, T)) * s)
    return {
        "x_words": packed_xT[0],
        "x_scales": packed_xT[1],
        "w1": (n((K, N)) / np.sqrt(K) / s).astype(np.float32),
        "w2": (n((K, N)) / np.sqrt(K) / s).astype(np.float32),
        "w3": (n((K, N)) / np.sqrt(K) / s).astype(np.float32),
        "offs": striped(np.random.permutation(T)[:S]),
        "cen": striped(np.random.permutation(S)[:V]),
        "pos1": striped(np.random.permutation(S)[:V]),
        "pos2": striped(np.random.permutation(S)[:V]),
        "pos3": striped(np.random.permutation(S)[:V]),
    }


def reference(x_words, x_scales, w1, w2, w3, offs, cen, pos1, pos2, pos3):
    xq = unpack_weight(x_words, x_scales)[:, unstriped(offs)]
    h = mxq(f64(w3), 0, "e4m3").T @ xq
    g = mxq(f64(w1), 0, "e4m3").T @ xq
    gc = g[:, unstriped(cen)]
    s = mxq(f64(w2), 0, "e4m3").T @ xq
    sc = s[:, unstriped(cen)]
    out_0 = relu(h[:, unstriped(pos1)] * gc + sc) + relu(h[:, unstriped(pos2)] * gc + sc) + relu(h[:, unstriped(pos3)] * gc + sc)
    return (out_0,) + planes(out_0)

@@ -1,0 +1,173 @@
+from contextlib import ExitStack
+
+import concourse.mybir as mybir
+from concourse.masks import make_identity
+
+K, T, S, V, N = 512, 1024, 512, 256, 512
+FLOPS = 3 * 2 * K * N * S
+
+F32 = mybir.dt.float32
+BF16 = mybir.dt.bfloat16
+I32 = mybir.dt.int32
+U32 = mybir.dt.uint32
+U16 = mybir.dt.uint16
+U8 = mybir.dt.uint8
+FP8X4 = mybir.dt.float8_e4m3fn_x4
+MULT = mybir.AluOpType.mult
+RELU = mybir.ActivationFunctionType.Relu
+
+P = 128
+PACK = 4
+HALF = N // 2
+
+
+def tile_picked_filmg_relu_po_kernel(
+    tc, x_words, x_scales, w1, w2, w3, offs, cen, pos1, pos2, pos3, out_0, out_1, out_2
+):
+    nc = tc.nc
+    with ExitStack() as ctx:
+        keep = ctx.enter_context(tc.tile_pool(name="keep", bufs=1))
+        prods = ctx.enter_context(tc.tile_pool(name="prods", bufs=9))
+        rects = ctx.enter_context(tc.tile_pool(name="rects", bufs=6))
+        mm_ps = ctx.enter_context(tc.psum_pool(name="mm_ps", bufs=3))
+        fw_ps = ctx.enter_context(tc.psum_pool(name="fw_ps", bufs=3))
+        bk_ps = ctx.enter_context(tc.psum_pool(name="bk_ps", bufs=2))
+
+        def load_list(src, name):
+            lst = keep.tile(list(src.shape), U16, name=name)
+            nc.sync.dma_start(lst[:], src)
+            return lst
+
+        def load_half(w, half, name):
+            raw = keep.tile([P, PACK, HALF], F32, name=name)
+            nc.sync.dma_start(raw[:], w.rearrange("(p j) c -> p j c", j=PACK)[:, :, half * HALF : (half + 1) * HALF])
+            return raw
+
+        offs_l = load_list(offs, "offs_l")
+        xs_rows = keep.tile([P, T // 4], I32, name="xs_rows")
+        for q in range(4):
+            nc.scalar.dma_start(xs_rows[32 * q : 32 * q + 4, :], x_scales[0, 4 * q : 4 * q + 4, :].bitcast(I32))
+        xs = keep.tile([P, T], U8, name="xs")
+        nc.gpsimd.memset(xs[:].bitcast(I32), 0)
+        for q in range(4):
+            nc.vector.tensor_copy(xs[32 * q : 32 * q + 4, :].bitcast(I32), xs_rows[32 * q : 32 * q + 4, :])
+        xw = keep.tile([P, T], U32, name="xw")
+        nc.sync.dma_start(xw[:].bitcast(I32), x_words[0].rearrange("p n t -> p (n t)").bitcast(I32))
+        raw_g = [load_half(w1, h, "raw_g%d" % h) for h in range(2)]
+        raw_s0 = load_half(w2, 0, "raw_s0")
+        cen_l = load_list(cen, "cen_l")
+        raw_s = [raw_s0, load_half(w2, 1, "raw_s1")]
+        raw_h = [load_half(w3, h, "raw_h%d" % h) for h in range(2)]
+        pos_l = [load_list(src, "pos_l%d" % d) for d, src in enumerate((pos1, pos2, pos3))]
+
+        seed = keep.tile([P, P], F32, name="seed")
+        make_identity(nc, seed[:])
+        ident = keep.tile([P, P], F32, name="ident")
+        nc.scalar.activation(ident[:], seed[:], RELU)
+
+        xg_w = keep.tile([P, S], U32, name="xg_w", align_bytes=64)
+        nc.vector.tensor_copy(xg_w[:], xw[:].indirect(offs_l[:]))
+        xg_s = keep.tile([P, S], U8, name="xg_s", align_bytes=64)
+        nc.vector.tensor_copy(xg_s[:], xs[:].indirect(offs_l[:]))
+
+        def operand(name):
+            return (
+                keep.tile([P, N * PACK], BF16, name=name + "_bf", align_bytes=64),
+                keep.tile([P, N], U32, name=name + "_codes", align_bytes=64),
+                keep.tile([P, N], U8, name=name + "_scales", align_bytes=64),
+            )
+
+        def cast(copy, op, raw, half):
+            dst = op[0][:].rearrange("p (t m j) -> p m j t", t=PACK, j=PACK)[:, half * 64 : (half + 1) * 64]
+            copy(dst, raw[half][:].rearrange("p j (m t) -> p m j t", t=PACK))
+
+        def quantize(op, t0, t1):
+            nc.vector.quantize_mx(
+                out=op[1][:, t0 * P : t1 * P].bitcast(FP8X4),
+                scales=op[2][:, t0 * P : t1 * P],
+                in_=op[0][:, t0 * P * PACK : t1 * P * PACK],
+            )
+
+        def product(op, t, name):
+            acc = mm_ps.tile([P, S], F32, name="acc")
+            cols = slice(t * P, (t + 1) * P)
+            nc.tensor.matmul_mx(
+                out=acc[:], lhsT=op[1][:, cols].bitcast(FP8X4), lhsT_scale=op[2][:, cols],
+                rhs=xg_w[:].bitcast(FP8X4), rhs_scale=xg_s[:], start=True, stop=True,
+            )
+            res = keep.tile([P, S], F32, name="%s%d" % (name, t))
+            nc.scalar.copy(res[:], acc[:])
+            return res
+
+        def at_targets(res, name):
+            picked = keep.tile([P, V], F32, name=name)
+            nc.vector.tensor_copy(picked[:], res[:].indirect(cen_l[:]))
+            return picked
+
+        def messages(h, gc):
+            out = []
+            for d in range(3):
+                prod = prods.tile([P, V], F32, name="prod")
+                nc.vector.tensor_tensor(prod[:], h[:].indirect(pos_l[d][:]), gc[:], MULT)
+                out.append(prod)
+            return out
+
+        y = keep.tile([P, PACK, V], F32, name="y")
+        out_rows = out_0.rearrange("(p t) v -> p t v", t=PACK)
+
+        def finish(t, prod, sc):
+            rect = []
+            for d in range(3):
+                fw = fw_ps.tile([P, 2, P], F32, name="fw")
+                for b in range(2):
+                    cols = slice(b * P, (b + 1) * P)
+                    nc.tensor.matmul(fw[:, b, :], sc[:, cols], ident[:], start=True, stop=False, is_transpose=True)
+                    nc.tensor.matmul(fw[:, b, :], prod[d][:, cols], ident[:], start=False, stop=True, is_transpose=True)
+                r = rects.tile([P, 2, P], F32, name="r")
+                nc.scalar.activation(r[:], fw[:], RELU)
+                rect.append(r)
+            bk = bk_ps.tile([P, V], F32, name="bk")
+            for b in range(2):
+                for d in range(3):
+                    nc.tensor.matmul(bk[:, b * P : (b + 1) * P], rect[d][:, b, :], ident[:], start=(d == 0), stop=(d == 2), is_transpose=True)
+            nc.scalar.copy(y[:, t, :], bk[:])
+            nc.sync.dma_start(out_rows[:, t, :], y[:, t, :])
+
+        op_g, op_h, op_s = operand("g"), operand("h"), operand("s")
+        cast(nc.scalar.copy, op_g, raw_g, 0)
+        cast(nc.vector.tensor_copy, op_g, raw_g, 1)
+        quantize(op_g, 0, 1)
+        quantize(op_g, 1, 2)
+        quantize(op_g, 2, 4)
+        g = [product(op_g, 0, "g")]
+        cast(nc.vector.tensor_copy, op_s, raw_s, 0)
+        cast(nc.scalar.copy, op_s, raw_s, 1)
+        quantize(op_s, 0, 2)
+        quantize(op_s, 2, 4)
+        g.extend(product(op_g, t, "g") for t in range(1, 4))
+        cast(nc.vector.tensor_copy, op_h, raw_h, 0)
+        cast(nc.scalar.copy, op_h, raw_h, 1)
+        quantize(op_h, 0, 1)
+        quantize(op_h, 1, 2)
+        quantize(op_h, 2, 4)
+        s, h = [], []
+        for t in range(4):
+            s.append(product(op_s, t, "s"))
+            h.append(product(op_h, t, "h"))
+        gc = [at_targets(g[t], "gc%d" % t) for t in range(4)]
+        for t in range(4):
+            sc = at_targets(s[t], "sc%d" % t)
+            finish(t, messages(h[t], gc[t]), sc)
+
+        y_bf = keep.tile([P, V * PACK], BF16, name="y_bf", align_bytes=64)
+        nc.vector.tensor_copy(
+            y_bf[:].rearrange("p (c i t) -> p c t i", i=4, t=PACK),
+            y[:].rearrange("p t (c i) -> p c t i", i=4),
+        )
+        y_codes = keep.tile([P, V], U32, name="y_codes", align_bytes=64)
+        y_scales = keep.tile([P, V], U8, name="y_scales", align_bytes=64)
+        nc.vector.quantize_mx(out=y_codes[:].bitcast(FP8X4), scales=y_scales[:], in_=y_bf[:])
+        nc.sync.dma_start(out_1[0].rearrange("p c r -> p (c r)").bitcast(I32), y_codes[:].bitcast(I32))
+        for q in range(4):
+            queue = nc.scalar if q % 2 else nc.sync
+            queue.dma_start(out_2[0, 4 * q : 4 * q + 4, :].bitcast(I32), y_scales[32 * q : 32 * q + 4, :].bitcast(I32))

@@ -14,6 +14,8 @@ U16 = mybir.dt.uint16
 U8 = mybir.dt.uint8
 FP8X4 = mybir.dt.float8_e4m3fn_x4
 MULT = mybir.AluOpType.mult
+ADD = mybir.AluOpType.add
+MAX = mybir.AluOpType.max
 RELU = mybir.ActivationFunctionType.Relu
 
 P = 128
@@ -44,15 +46,11 @@ def tile_picked_filmg_relu_po_kernel(
             return raw
 
         offs_l = load_list(offs, "offs_l")
-        xs_rows = keep.tile([P, T // 4], I32, name="xs_rows")
-        for q in range(4):
-            nc.scalar.dma_start(xs_rows[32 * q : 32 * q + 4, :], x_scales[0, 4 * q : 4 * q + 4, :].bitcast(I32))
-        xs = keep.tile([P, T], U8, name="xs")
-        nc.gpsimd.memset(xs[:].bitcast(I32), 0)
-        for q in range(4):
-            nc.vector.tensor_copy(xs[32 * q : 32 * q + 4, :].bitcast(I32), xs_rows[32 * q : 32 * q + 4, :])
         xw = keep.tile([P, T], U32, name="xw")
         nc.sync.dma_start(xw[:].bitcast(I32), x_words[0].rearrange("p n t -> p (n t)").bitcast(I32))
+        xs_rows = keep.tile([P, T // 4], I32, name="xs_rows")
+        for q in range(4):
+            nc.sync.dma_start(xs_rows[32 * q : 32 * q + 4, :], x_scales[0, 4 * q : 4 * q + 4, :].bitcast(I32))
         raw_g = [load_half(w1, h, "raw_g%d" % h) for h in range(2)]
         raw_s0 = load_half(w2, 0, "raw_s0")
         cen_l = load_list(cen, "cen_l")
@@ -67,12 +65,16 @@ def tile_picked_filmg_relu_po_kernel(
 
         xg_w = keep.tile([P, S], U32, name="xg_w", align_bytes=64)
         nc.vector.tensor_copy(xg_w[:], xw[:].indirect(offs_l[:]))
+        xs = keep.tile([P, T], U8, name="xs")
+        nc.gpsimd.memset(xs[:].bitcast(I32), 0)
+        for q in range(4):
+            nc.vector.tensor_copy(xs[32 * q : 32 * q + 4, :].bitcast(I32), xs_rows[32 * q : 32 * q + 4, :])
         xg_s = keep.tile([P, S], U8, name="xg_s", align_bytes=64)
         nc.vector.tensor_copy(xg_s[:], xs[:].indirect(offs_l[:]))
 
-        def operand(name):
+        def operand(name, stage):
             return (
-                keep.tile([P, N * PACK], BF16, name=name + "_bf", align_bytes=64),
+                keep.tile([P, N * PACK], BF16, name=stage, align_bytes=64),
                 keep.tile([P, N], U32, name=name + "_codes", align_bytes=64),
                 keep.tile([P, N], U8, name=name + "_scales", align_bytes=64),
             )
@@ -104,60 +106,76 @@ def tile_picked_filmg_relu_po_kernel(
             nc.vector.tensor_copy(picked[:], res[:].indirect(cen_l[:]))
             return picked
 
-        def messages(h, gc):
-            out = []
-            for d in range(3):
-                prod = prods.tile([P, V], F32, name="prod")
-                nc.vector.tensor_tensor(prod[:], h[:].indirect(pos_l[d][:]), gc[:], MULT)
-                out.append(prod)
-            return out
+        def message(out, h, gc, d):
+            nc.vector.tensor_tensor(out, h[:].indirect(pos_l[d][:]), gc[:], MULT)
 
         y = keep.tile([P, PACK, V], F32, name="y")
         out_rows = out_0.rearrange("(p t) v -> p t v", t=PACK)
 
-        def finish(t, prod, sc):
+        def finish_with_tensor(t, h, gc, sc):
             rect = []
-            for d in range(3):
+            for d in range(2):
+                prod = prods.tile([P, V], F32, name="prod")
+                message(prod[:], h, gc, d)
                 fw = fw_ps.tile([P, 2, P], F32, name="fw")
                 for b in range(2):
                     cols = slice(b * P, (b + 1) * P)
                     nc.tensor.matmul(fw[:, b, :], sc[:, cols], ident[:], start=True, stop=False, is_transpose=True)
-                    nc.tensor.matmul(fw[:, b, :], prod[d][:, cols], ident[:], start=False, stop=True, is_transpose=True)
+                    nc.tensor.matmul(fw[:, b, :], prod[:, cols], ident[:], start=False, stop=True, is_transpose=True)
                 r = rects.tile([P, 2, P], F32, name="r")
                 nc.scalar.activation(r[:], fw[:], RELU)
                 rect.append(r)
             bk = bk_ps.tile([P, V], F32, name="bk")
             for b in range(2):
-                for d in range(3):
-                    nc.tensor.matmul(bk[:, b * P : (b + 1) * P], rect[d][:, b, :], ident[:], start=(d == 0), stop=(d == 2), is_transpose=True)
-            nc.scalar.copy(y[:, t, :], bk[:])
+                for d in range(2):
+                    nc.tensor.matmul(bk[:, b * P : (b + 1) * P], rect[d][:, b, :], ident[:], start=(d == 0), stop=(d == 1), is_transpose=True)
+            prod = prods.tile([P, V], F32, name="prod")
+            message(prod[:], h, gc, 2)
+            last = prods.tile([P, V], F32, name="last")
+            nc.vector.tensor_tensor(last[:], prod[:], sc[:], ADD)
+            nc.vector.scalar_tensor_tensor(y[:, t, :], last[:], 0.0, bk[:], MAX, ADD)
             nc.sync.dma_start(out_rows[:, t, :], y[:, t, :])
 
-        op_g, op_h, op_s = operand("g"), operand("h"), operand("s")
-        cast(nc.scalar.copy, op_g, raw_g, 0)
-        cast(nc.vector.tensor_copy, op_g, raw_g, 1)
-        quantize(op_g, 0, 1)
-        quantize(op_g, 1, 2)
-        quantize(op_g, 2, 4)
-        g = [product(op_g, 0, "g")]
-        cast(nc.vector.tensor_copy, op_s, raw_s, 0)
-        cast(nc.scalar.copy, op_s, raw_s, 1)
-        quantize(op_s, 0, 2)
-        quantize(op_s, 2, 4)
-        g.extend(product(op_g, t, "g") for t in range(1, 4))
-        cast(nc.vector.tensor_copy, op_h, raw_h, 0)
-        cast(nc.scalar.copy, op_h, raw_h, 1)
-        quantize(op_h, 0, 1)
-        quantize(op_h, 1, 2)
-        quantize(op_h, 2, 4)
-        s, h = [], []
-        for t in range(4):
-            s.append(product(op_s, t, "s"))
-            h.append(product(op_h, t, "h"))
+        def finish_without_tensor(t, h, gc, sc):
+            pair = keep.tile([P, 2, V], F32, name="pair")
+            for d in range(2):
+                message(pair[:, d, :], h, gc, d)
+            pair_u = keep.tile([P, 2, V], F32, name="pair_u")
+            nc.vector.tensor_tensor(pair_u[:], pair[:], sc[:].unsqueeze(1).to_broadcast([P, 2, V]), ADD)
+            pair_r = keep.tile([P, 2, V], F32, name="pair_r")
+            nc.scalar.activation(pair_r[:], pair_u[:], RELU)
+            prod = prods.tile([P, V], F32, name="prod")
+            message(prod[:], h, gc, 2)
+            last = prods.tile([P, V], F32, name="last")
+            nc.vector.tensor_tensor(last[:], prod[:], sc[:], ADD)
+            both = keep.tile([P, V], F32, name="both")
+            nc.vector.tensor_tensor(both[:], pair_r[:, 0, :], pair_r[:, 1, :], ADD)
+            nc.vector.scalar_tensor_tensor(y[:, t, :], last[:], 0.0, both[:], MAX, ADD)
+            nc.sync.dma_start(out_rows[:, t, :], y[:, t, :])
+
+        def prepare(name, stage, raw):
+            op = operand(name, stage)
+            cast(nc.scalar.copy, op, raw, 0)
+            cast(nc.vector.tensor_copy, op, raw, 1)
+            quantize(op, 0, 1)
+            quantize(op, 1, 2)
+            quantize(op, 2, 4)
+            return op
+
+        op_g = prepare("g", "stage_a", raw_g)
+        op_s = prepare("s", "stage_b", raw_s)
+        g = [product(op_g, t, "g") for t in range(4)]
+        op_h = prepare("h", "stage_b", raw_h)
         gc = [at_targets(g[t], "gc%d" % t) for t in range(4)]
+        s = [product(op_s, 0, "s")]
+        h = [product(op_h, 0, "h")]
         for t in range(4):
+            if t + 1 < 4:
+                s.append(product(op_s, t + 1, "s"))
+                h.append(product(op_h, t + 1, "h"))
             sc = at_targets(s[t], "sc%d" % t)
-            finish(t, messages(h[t], gc[t]), sc)
+            finish = finish_with_tensor if t < 3 else finish_without_tensor
+            finish(t, h[t], gc[t], sc)
 
         y_bf = keep.tile([P, V * PACK], BF16, name="y_bf", align_bytes=64)
         nc.vector.tensor_copy(

@@ -46,11 +46,11 @@ def tile_picked_filmg_relu_po_kernel(
             return raw
 
         offs_l = load_list(offs, "offs_l")
-        xw = keep.tile([P, T], U32, name="xw")
-        nc.sync.dma_start(xw[:].bitcast(I32), x_words[0].rearrange("p n t -> p (n t)").bitcast(I32))
         xs_rows = keep.tile([P, T // 4], I32, name="xs_rows")
         for q in range(4):
             nc.sync.dma_start(xs_rows[32 * q : 32 * q + 4, :], x_scales[0, 4 * q : 4 * q + 4, :].bitcast(I32))
+        xw = keep.tile([P, T], U32, name="xw")
+        nc.sync.dma_start(xw[:].bitcast(I32), x_words[0].rearrange("p n t -> p (n t)").bitcast(I32))
         raw_g = [load_half(w1, h, "raw_g%d" % h) for h in range(2)]
         raw_s0 = load_half(w2, 0, "raw_s0")
         cen_l = load_list(cen, "cen_l")
@@ -63,25 +63,25 @@ def tile_picked_filmg_relu_po_kernel(
         ident = keep.tile([P, P], F32, name="ident")
         nc.scalar.activation(ident[:], seed[:], RELU)
 
-        xg_w = keep.tile([P, S], U32, name="xg_w", align_bytes=64)
-        nc.vector.tensor_copy(xg_w[:], xw[:].indirect(offs_l[:]))
         xs = keep.tile([P, T], U8, name="xs")
         nc.gpsimd.memset(xs[:].bitcast(I32), 0)
         for q in range(4):
             nc.vector.tensor_copy(xs[32 * q : 32 * q + 4, :].bitcast(I32), xs_rows[32 * q : 32 * q + 4, :])
         xg_s = keep.tile([P, S], U8, name="xg_s", align_bytes=64)
         nc.vector.tensor_copy(xg_s[:], xs[:].indirect(offs_l[:]))
+        xg_w = keep.tile([P, S], U32, name="xg_w", align_bytes=64)
+        nc.vector.tensor_copy(xg_w[:], xw[:].indirect(offs_l[:]))
 
         def operand(name, stage):
             return (
-                keep.tile([P, N * PACK], BF16, name=stage, align_bytes=64),
+                keep.tile([P, N * PACK], BF16, name=name + "_stage", tag=stage, align_bytes=64),
                 keep.tile([P, N], U32, name=name + "_codes", align_bytes=64),
                 keep.tile([P, N], U8, name=name + "_scales", align_bytes=64),
             )
 
         def cast(copy, op, raw, half):
-            dst = op[0][:].rearrange("p (t m j) -> p m j t", t=PACK, j=PACK)[:, half * 64 : (half + 1) * 64]
-            copy(dst, raw[half][:].rearrange("p j (m t) -> p m j t", t=PACK))
+            dst = op[0][:].rearrange("p (t m j) -> p m t j", t=PACK, j=PACK)[:, half * 64 : (half + 1) * 64]
+            copy(dst, raw[half][:].rearrange("p j (m t) -> p m t j", t=PACK))
 
         def quantize(op, t0, t1):
             nc.vector.quantize_mx(
@@ -90,14 +90,14 @@ def tile_picked_filmg_relu_po_kernel(
                 in_=op[0][:, t0 * P * PACK : t1 * P * PACK],
             )
 
-        def product(op, t, name):
+        def product(op, t, name, tag=None):
             acc = mm_ps.tile([P, S], F32, name="acc")
             cols = slice(t * P, (t + 1) * P)
             nc.tensor.matmul_mx(
                 out=acc[:], lhsT=op[1][:, cols].bitcast(FP8X4), lhsT_scale=op[2][:, cols],
                 rhs=xg_w[:].bitcast(FP8X4), rhs_scale=xg_s[:], start=True, stop=True,
             )
-            res = keep.tile([P, S], F32, name="%s%d" % (name, t))
+            res = keep.tile([P, S], F32, name="%s%d" % (name, t), tag=tag or "%s%d" % (name, t), align_bytes=64)
             nc.scalar.copy(res[:], acc[:])
             return res
 
@@ -112,9 +112,9 @@ def tile_picked_filmg_relu_po_kernel(
         y = keep.tile([P, PACK, V], F32, name="y")
         out_rows = out_0.rearrange("(p t) v -> p t v", t=PACK)
 
-        def finish_with_tensor(t, h, gc, sc):
+        def finish_with_tensor(t, h, gc, sc, n):
             rect = []
-            for d in range(2):
+            for d in range(n):
                 prod = prods.tile([P, V], F32, name="prod")
                 message(prod[:], h, gc, d)
                 fw = fw_ps.tile([P, 2, P], F32, name="fw")
@@ -127,13 +127,16 @@ def tile_picked_filmg_relu_po_kernel(
                 rect.append(r)
             bk = bk_ps.tile([P, V], F32, name="bk")
             for b in range(2):
-                for d in range(2):
-                    nc.tensor.matmul(bk[:, b * P : (b + 1) * P], rect[d][:, b, :], ident[:], start=(d == 0), stop=(d == 1), is_transpose=True)
-            prod = prods.tile([P, V], F32, name="prod")
-            message(prod[:], h, gc, 2)
-            last = prods.tile([P, V], F32, name="last")
-            nc.vector.tensor_tensor(last[:], prod[:], sc[:], ADD)
-            nc.vector.scalar_tensor_tensor(y[:, t, :], last[:], 0.0, bk[:], MAX, ADD)
+                for d in range(n):
+                    nc.tensor.matmul(bk[:, b * P : (b + 1) * P], rect[d][:, b, :], ident[:], start=(d == 0), stop=(d == n - 1), is_transpose=True)
+            if n == 3:
+                nc.scalar.copy(y[:, t, :], bk[:])
+            else:
+                prod = prods.tile([P, V], F32, name="prod")
+                message(prod[:], h, gc, 2)
+                last = prods.tile([P, V], F32, name="last")
+                nc.vector.tensor_tensor(last[:], prod[:], sc[:], ADD)
+                nc.vector.scalar_tensor_tensor(y[:, t, :], last[:], 0.0, bk[:], MAX, ADD)
             nc.sync.dma_start(out_rows[:, t, :], y[:, t, :])
 
         def finish_without_tensor(t, h, gc, sc):
@@ -150,22 +153,22 @@ def tile_picked_filmg_relu_po_kernel(
             nc.vector.tensor_tensor(last[:], prod[:], sc[:], ADD)
             both = keep.tile([P, V], F32, name="both")
             nc.vector.tensor_tensor(both[:], pair_r[:, 0, :], pair_r[:, 1, :], ADD)
-            nc.vector.scalar_tensor_tensor(y[:, t, :], last[:], 0.0, both[:], MAX, ADD)
+            for cols in (slice(0, P), slice(P, V)):
+                nc.vector.scalar_tensor_tensor(y[:, t, cols], last[:, cols], 0.0, both[:, cols], MAX, ADD)
             nc.sync.dma_start(out_rows[:, t, :], y[:, t, :])
 
-        def prepare(name, stage, raw):
+        def prepare(name, stage, raw, pieces):
             op = operand(name, stage)
             cast(nc.scalar.copy, op, raw, 0)
             cast(nc.vector.tensor_copy, op, raw, 1)
-            quantize(op, 0, 1)
-            quantize(op, 1, 2)
-            quantize(op, 2, 4)
+            for t0, t1 in pieces:
+                quantize(op, t0, t1)
             return op
 
-        op_g = prepare("g", "stage_a", raw_g)
-        op_s = prepare("s", "stage_b", raw_s)
+        op_g = prepare("g", "stage_a", raw_g, ((0, 1), (1, 2), (2, 4)))
+        op_s = prepare("s", "stage_b", raw_s, ((0, 4),))
         g = [product(op_g, t, "g") for t in range(4)]
-        op_h = prepare("h", "stage_b", raw_h)
+        op_h = prepare("h", "stage_b", raw_h, ((0, 2), (2, 4)))
         gc = [at_targets(g[t], "gc%d" % t) for t in range(4)]
         s = [product(op_s, 0, "s")]
         h = [product(op_h, 0, "h")]
@@ -174,17 +177,22 @@ def tile_picked_filmg_relu_po_kernel(
                 s.append(product(op_s, t + 1, "s"))
                 h.append(product(op_h, t + 1, "h"))
             sc = at_targets(s[t], "sc%d" % t)
-            finish = finish_with_tensor if t < 3 else finish_without_tensor
-            finish(t, h[t], gc[t], sc)
+            if t < 3:
+                finish_with_tensor(t, h[t], gc[t], sc, 3 if t < 2 else 2)
+            else:
+                finish_without_tensor(t, h[t], gc[t], sc)
 
-        y_bf = keep.tile([P, V * PACK], BF16, name="y_bf", align_bytes=64)
-        nc.vector.tensor_copy(
-            y_bf[:].rearrange("p (c i t) -> p c t i", i=4, t=PACK),
-            y[:].rearrange("p t (c i) -> p c t i", i=4),
-        )
         y_codes = keep.tile([P, V], U32, name="y_codes", align_bytes=64)
         y_scales = keep.tile([P, V], U8, name="y_scales", align_bytes=64)
-        nc.vector.quantize_mx(out=y_codes[:].bitcast(FP8X4), scales=y_scales[:], in_=y_bf[:])
+        y_bf = [keep.tile([P, P * PACK], BF16, name="y_bf%d" % b, align_bytes=64) for b in range(2)]
+        for b in range(2):
+            nc.vector.tensor_copy(
+                y_bf[b][:].rearrange("p (c i t) -> p c t i", i=4, t=PACK),
+                y[:, :, b * P : (b + 1) * P].rearrange("p t (c i) -> p c t i", i=4),
+            )
+        for b in range(2):
+            cols = slice(b * P, (b + 1) * P)
+            nc.vector.quantize_mx(out=y_codes[:, cols].bitcast(FP8X4), scales=y_scales[:, cols], in_=y_bf[b][:])
         nc.sync.dma_start(out_1[0].rearrange("p c r -> p (c r)").bitcast(I32), y_codes[:].bitcast(I32))
         for q in range(4):
             queue = nc.scalar if q % 2 else nc.sync

@@ -29,11 +29,11 @@ def tile_picked_filmg_relu_po_kernel(
     nc = tc.nc
     with ExitStack() as ctx:
         keep = ctx.enter_context(tc.tile_pool(name="keep", bufs=1))
-        prods = ctx.enter_context(tc.tile_pool(name="prods", bufs=9))
+        prods = ctx.enter_context(tc.tile_pool(name="prods", bufs=10))
         rects = ctx.enter_context(tc.tile_pool(name="rects", bufs=6))
-        mm_ps = ctx.enter_context(tc.psum_pool(name="mm_ps", bufs=3))
+        mm_ps = ctx.enter_context(tc.psum_pool(name="mm_ps", bufs=4))
         fw_ps = ctx.enter_context(tc.psum_pool(name="fw_ps", bufs=3))
-        bk_ps = ctx.enter_context(tc.psum_pool(name="bk_ps", bufs=2))
+        bk_ps = ctx.enter_context(tc.psum_pool(name="bk_ps", bufs=1))
 
         def load_list(src, name):
             lst = keep.tile(list(src.shape), U16, name=name)
@@ -145,51 +145,64 @@ def tile_picked_filmg_relu_po_kernel(
                 message(pair[:, d, :], h, gc, d)
             pair_u = keep.tile([P, 2, V], F32, name="pair_u")
             nc.vector.tensor_tensor(pair_u[:], pair[:], sc[:].unsqueeze(1).to_broadcast([P, 2, V]), ADD)
-            pair_r = keep.tile([P, 2, V], F32, name="pair_r")
-            nc.scalar.activation(pair_r[:], pair_u[:], RELU)
+            first = keep.tile([P, V], F32, name="first")
+            nc.vector.tensor_scalar(first[:], pair_u[:, 0, :], 0.0, None, MAX)
             prod = prods.tile([P, V], F32, name="prod")
             message(prod[:], h, gc, 2)
+            both = keep.tile([P, V], F32, name="both")
+            nc.vector.scalar_tensor_tensor(both[:], pair_u[:, 1, :], 0.0, first[:], MAX, ADD)
             last = prods.tile([P, V], F32, name="last")
             nc.vector.tensor_tensor(last[:], prod[:], sc[:], ADD)
-            both = keep.tile([P, V], F32, name="both")
-            nc.vector.tensor_tensor(both[:], pair_r[:, 0, :], pair_r[:, 1, :], ADD)
             for cols in (slice(0, P), slice(P, V)):
                 nc.vector.scalar_tensor_tensor(y[:, t, cols], last[:, cols], 0.0, both[:, cols], MAX, ADD)
             nc.sync.dma_start(out_rows[:, t, :], y[:, t, :])
 
-        def prepare(name, stage, raw, pieces):
-            op = operand(name, stage)
-            cast(nc.scalar.copy, op, raw, 0)
-            cast(nc.vector.tensor_copy, op, raw, 1)
+        def quantize_all(op, pieces):
             for t0, t1 in pieces:
                 quantize(op, t0, t1)
-            return op
-
-        op_g = prepare("g", "stage_a", raw_g, ((0, 1), (1, 2), (2, 4)))
-        op_s = prepare("s", "stage_b", raw_s, ((0, 4),))
-        g = [product(op_g, t, "g") for t in range(4)]
-        op_h = prepare("h", "stage_b", raw_h, ((0, 2), (2, 4)))
-        gc = [at_targets(g[t], "gc%d" % t) for t in range(4)]
-        s = [product(op_s, 0, "s")]
-        h = [product(op_h, 0, "h")]
-        for t in range(4):
-            if t + 1 < 4:
-                s.append(product(op_s, t + 1, "s"))
-                h.append(product(op_h, t + 1, "h"))
-            sc = at_targets(s[t], "sc%d" % t)
-            if t < 3:
-                finish_with_tensor(t, h[t], gc[t], sc, 3 if t < 2 else 2)
-            else:
-                finish_without_tensor(t, h[t], gc[t], sc)
 
         y_codes = keep.tile([P, V], U32, name="y_codes", align_bytes=64)
         y_scales = keep.tile([P, V], U8, name="y_scales", align_bytes=64)
         y_bf = [keep.tile([P, P * PACK], BF16, name="y_bf%d" % b, align_bytes=64) for b in range(2)]
-        for b in range(2):
-            nc.vector.tensor_copy(
-                y_bf[b][:].rearrange("p (c i t) -> p c t i", i=4, t=PACK),
-                y[:, :, b * P : (b + 1) * P].rearrange("p t (c i) -> p c t i", i=4),
-            )
+
+        def round_pair(copy, t0):
+            for b in range(2):
+                copy(
+                    y_bf[b][:].rearrange("p (c i t) -> p c t i", i=4, t=PACK)[:, :, t0 : t0 + 2, :],
+                    y[:, t0 : t0 + 2, b * P : (b + 1) * P].rearrange("p t (c i) -> p c t i", i=4),
+                )
+
+        op_g = operand("g", "stage_a")
+        cast(nc.scalar.copy, op_g, raw_g, 0)
+        cast(nc.vector.tensor_copy, op_g, raw_g, 1)
+        quantize_all(op_g, ((0, 1), (1, 2), (2, 4)))
+        op_s = operand("s", "stage_b")
+        cast(nc.scalar.copy, op_s, raw_s, 0)
+        cast(nc.vector.tensor_copy, op_s, raw_s, 1)
+        quantize_all(op_s, ((0, 4),))
+        g = [product(op_g, t, "g") for t in range(3)]
+        op_h = operand("h", "stage_b")
+        cast(nc.scalar.copy, op_h, raw_h, 0)
+        cast(nc.scalar.copy, op_h, raw_h, 1)
+        quantize_all(op_h, ((0, 1), (1, 2), (2, 4)))
+        s = [product(op_s, 0, "s")]
+        h = [product(op_h, 0, "h")]
+        g.append(product(op_g, 3, "g"))
+        gc = [at_targets(g[t], "gc%d" % t) for t in range(4)]
+        s.append(product(op_s, 1, "s"))
+        h.append(product(op_h, 1, "h"))
+        for t in range(4):
+            if t + 2 < 4:
+                s.append(product(op_s, t + 2, "s"))
+                h.append(product(op_h, t + 2, "h"))
+            sc = at_targets(s[t], "sc%d" % t)
+            if t < 3:
+                finish_with_tensor(t, h[t], gc[t], sc, 3)
+            else:
+                finish_without_tensor(t, h[t], gc[t], sc)
+            if t == 1:
+                round_pair(nc.scalar.copy, 0)
+        round_pair(nc.vector.tensor_copy, 2)
         for b in range(2):
             cols = slice(b * P, (b + 1) * P)
             nc.vector.quantize_mx(out=y_codes[:, cols].bitcast(FP8X4), scales=y_scales[:, cols], in_=y_bf[b][:])

from contextlib import ExitStack

import concourse.mybir as mybir
from concourse.masks import make_identity

K, T, S, V, N = 512, 1024, 512, 256, 512
FLOPS = 3 * 2 * K * N * S

F32 = mybir.dt.float32
BF16 = mybir.dt.bfloat16
I32 = mybir.dt.int32
U32 = mybir.dt.uint32
U16 = mybir.dt.uint16
U8 = mybir.dt.uint8
FP8X4 = mybir.dt.float8_e4m3fn_x4
MULT = mybir.AluOpType.mult
ADD = mybir.AluOpType.add
MAX = mybir.AluOpType.max
RELU = mybir.ActivationFunctionType.Relu

P = 128
PACK = 4
HALF = N // 2


def tile_picked_filmg_relu_po_kernel(
    tc, x_words, x_scales, w1, w2, w3, offs, cen, pos1, pos2, pos3, out_0, out_1, out_2
):
    nc = tc.nc
    with ExitStack() as ctx:
        keep = ctx.enter_context(tc.tile_pool(name="keep", bufs=1))
        prods = ctx.enter_context(tc.tile_pool(name="prods", bufs=10))
        rects = ctx.enter_context(tc.tile_pool(name="rects", bufs=6))
        mm_ps = ctx.enter_context(tc.psum_pool(name="mm_ps", bufs=4))
        fw_ps = ctx.enter_context(tc.psum_pool(name="fw_ps", bufs=3))
        bk_ps = ctx.enter_context(tc.psum_pool(name="bk_ps", bufs=1))

        def load_list(src, name):
            lst = keep.tile(list(src.shape), U16, name=name)
            nc.sync.dma_start(lst[:], src)
            return lst

        def load_half(w, half, name):
            raw = keep.tile([P, PACK, HALF], F32, name=name)
            nc.sync.dma_start(raw[:], w.rearrange("(p j) c -> p j c", j=PACK)[:, :, half * HALF : (half + 1) * HALF])
            return raw

        offs_l = load_list(offs, "offs_l")
        xs_rows = keep.tile([P, T // 4], I32, name="xs_rows")
        for q in range(4):
            nc.sync.dma_start(xs_rows[32 * q : 32 * q + 4, :], x_scales[0, 4 * q : 4 * q + 4, :].bitcast(I32))
        xw = keep.tile([P, T], U32, name="xw")
        nc.sync.dma_start(xw[:].bitcast(I32), x_words[0].rearrange("p n t -> p (n t)").bitcast(I32))
        raw_g = [load_half(w1, h, "raw_g%d" % h) for h in range(2)]
        raw_s0 = load_half(w2, 0, "raw_s0")
        cen_l = load_list(cen, "cen_l")
        raw_s = [raw_s0, load_half(w2, 1, "raw_s1")]
        raw_h = [load_half(w3, h, "raw_h%d" % h) for h in range(2)]
        pos_l = [load_list(src, "pos_l%d" % d) for d, src in enumerate((pos1, pos2, pos3))]

        seed = keep.tile([P, P], F32, name="seed")
        make_identity(nc, seed[:])
        ident = keep.tile([P, P], F32, name="ident")
        nc.scalar.activation(ident[:], seed[:], RELU)

        xs = keep.tile([P, T], U8, name="xs")
        nc.gpsimd.memset(xs[:].bitcast(I32), 0)
        for q in range(4):
            nc.vector.tensor_copy(xs[32 * q : 32 * q + 4, :].bitcast(I32), xs_rows[32 * q : 32 * q + 4, :])
        xg_s = keep.tile([P, S], U8, name="xg_s", align_bytes=64)
        nc.vector.tensor_copy(xg_s[:], xs[:].indirect(offs_l[:]))
        xg_w = keep.tile([P, S], U32, name="xg_w", align_bytes=64)
        nc.vector.tensor_copy(xg_w[:], xw[:].indirect(offs_l[:]))

        def operand(name, stage):
            return (
                keep.tile([P, N * PACK], BF16, name=name + "_stage", tag=stage, align_bytes=64),
                keep.tile([P, N], U32, name=name + "_codes", align_bytes=64),
                keep.tile([P, N], U8, name=name + "_scales", align_bytes=64),
            )

        def cast(copy, op, raw, half):
            dst = op[0][:].rearrange("p (t m j) -> p m t j", t=PACK, j=PACK)[:, half * 64 : (half + 1) * 64]
            copy(dst, raw[half][:].rearrange("p j (m t) -> p m t j", t=PACK))

        def quantize(op, t0, t1):
            nc.vector.quantize_mx(
                out=op[1][:, t0 * P : t1 * P].bitcast(FP8X4),
                scales=op[2][:, t0 * P : t1 * P],
                in_=op[0][:, t0 * P * PACK : t1 * P * PACK],
            )

        def product(op, t, name, tag=None):
            acc = mm_ps.tile([P, S], F32, name="acc")
            cols = slice(t * P, (t + 1) * P)
            nc.tensor.matmul_mx(
                out=acc[:], lhsT=op[1][:, cols].bitcast(FP8X4), lhsT_scale=op[2][:, cols],
                rhs=xg_w[:].bitcast(FP8X4), rhs_scale=xg_s[:], start=True, stop=True,
            )
            res = keep.tile([P, S], F32, name="%s%d" % (name, t), tag=tag or "%s%d" % (name, t), align_bytes=64)
            nc.scalar.copy(res[:], acc[:])
            return res

        def at_targets(res, name):
            picked = keep.tile([P, V], F32, name=name)
            nc.vector.tensor_copy(picked[:], res[:].indirect(cen_l[:]))
            return picked

        def message(out, h, gc, d):
            nc.vector.tensor_tensor(out, h[:].indirect(pos_l[d][:]), gc[:], MULT)

        y = keep.tile([P, PACK, V], F32, name="y")
        out_rows = out_0.rearrange("(p t) v -> p t v", t=PACK)

        def finish_with_tensor(t, h, gc, sc, n):
            rect = []
            for d in range(n):
                prod = prods.tile([P, V], F32, name="prod")
                message(prod[:], h, gc, d)
                fw = fw_ps.tile([P, 2, P], F32, name="fw")
                for b in range(2):
                    cols = slice(b * P, (b + 1) * P)
                    nc.tensor.matmul(fw[:, b, :], sc[:, cols], ident[:], start=True, stop=False, is_transpose=True)
                    nc.tensor.matmul(fw[:, b, :], prod[:, cols], ident[:], start=False, stop=True, is_transpose=True)
                r = rects.tile([P, 2, P], F32, name="r")
                nc.scalar.activation(r[:], fw[:], RELU)
                rect.append(r)
            bk = bk_ps.tile([P, V], F32, name="bk")
            for b in range(2):
                for d in range(n):
                    nc.tensor.matmul(bk[:, b * P : (b + 1) * P], rect[d][:, b, :], ident[:], start=(d == 0), stop=(d == n - 1), is_transpose=True)
            if n == 3:
                nc.scalar.copy(y[:, t, :], bk[:])
            else:
                prod = prods.tile([P, V], F32, name="prod")
                message(prod[:], h, gc, 2)
                last = prods.tile([P, V], F32, name="last")
                nc.vector.tensor_tensor(last[:], prod[:], sc[:], ADD)
                nc.vector.scalar_tensor_tensor(y[:, t, :], last[:], 0.0, bk[:], MAX, ADD)
            nc.sync.dma_start(out_rows[:, t, :], y[:, t, :])

        def finish_without_tensor(t, h, gc, sc):
            pair = keep.tile([P, 2, V], F32, name="pair")
            for d in range(2):
                message(pair[:, d, :], h, gc, d)
            pair_u = keep.tile([P, 2, V], F32, name="pair_u")
            nc.vector.tensor_tensor(pair_u[:], pair[:], sc[:].unsqueeze(1).to_broadcast([P, 2, V]), ADD)
            first = keep.tile([P, V], F32, name="first")
            nc.vector.tensor_scalar(first[:], pair_u[:, 0, :], 0.0, None, MAX)
            prod = prods.tile([P, V], F32, name="prod")
            message(prod[:], h, gc, 2)
            both = keep.tile([P, V], F32, name="both")
            nc.vector.scalar_tensor_tensor(both[:], pair_u[:, 1, :], 0.0, first[:], MAX, ADD)
            last = prods.tile([P, V], F32, name="last")
            nc.vector.tensor_tensor(last[:], prod[:], sc[:], ADD)
            for cols in (slice(0, P), slice(P, V)):
                nc.vector.scalar_tensor_tensor(y[:, t, cols], last[:, cols], 0.0, both[:, cols], MAX, ADD)
            nc.sync.dma_start(out_rows[:, t, :], y[:, t, :])

        def quantize_all(op, pieces):
            for t0, t1 in pieces:
                quantize(op, t0, t1)

        y_codes = keep.tile([P, V], U32, name="y_codes", align_bytes=64)
        y_scales = keep.tile([P, V], U8, name="y_scales", align_bytes=64)
        y_bf = [keep.tile([P, P * PACK], BF16, name="y_bf%d" % b, align_bytes=64) for b in range(2)]

        def round_pair(copy, t0):
            for b in range(2):
                copy(
                    y_bf[b][:].rearrange("p (c i t) -> p c t i", i=4, t=PACK)[:, :, t0 : t0 + 2, :],
                    y[:, t0 : t0 + 2, b * P : (b + 1) * P].rearrange("p t (c i) -> p c t i", i=4),
                )

        op_g = operand("g", "stage_a")
        cast(nc.scalar.copy, op_g, raw_g, 0)
        cast(nc.vector.tensor_copy, op_g, raw_g, 1)
        quantize_all(op_g, ((0, 1), (1, 2), (2, 4)))
        op_s = operand("s", "stage_b")
        cast(nc.scalar.copy, op_s, raw_s, 0)
        cast(nc.vector.tensor_copy, op_s, raw_s, 1)
        quantize_all(op_s, ((0, 4),))
        g = [product(op_g, t, "g") for t in range(3)]
        op_h = operand("h", "stage_b")
        cast(nc.scalar.copy, op_h, raw_h, 0)
        cast(nc.scalar.copy, op_h, raw_h, 1)
        quantize_all(op_h, ((0, 1), (1, 2), (2, 4)))
        s = [product(op_s, 0, "s")]
        h = [product(op_h, 0, "h")]
        g.append(product(op_g, 3, "g"))
        gc = [at_targets(g[t], "gc%d" % t) for t in range(4)]
        s.append(product(op_s, 1, "s"))
        h.append(product(op_h, 1, "h"))
        for t in range(4):
            if t + 2 < 4:
                s.append(product(op_s, t + 2, "s"))
                h.append(product(op_h, t + 2, "h"))
            sc = at_targets(s[t], "sc%d" % t)
            if t < 3:
                finish_with_tensor(t, h[t], gc[t], sc, 3)
            else:
                finish_without_tensor(t, h[t], gc[t], sc)
            if t == 1:
                round_pair(nc.scalar.copy, 0)
        round_pair(nc.vector.tensor_copy, 2)
        for b in range(2):
            cols = slice(b * P, (b + 1) * P)
            nc.vector.quantize_mx(out=y_codes[:, cols].bitcast(FP8X4), scales=y_scales[:, cols], in_=y_bf[b][:])
        nc.sync.dma_start(out_1[0].rearrange("p c r -> p (c r)").bitcast(I32), y_codes[:].bitcast(I32))
        for q in range(4):
            queue = nc.scalar if q % 2 else nc.sync
            queue.dma_start(out_2[0, 4 * q : 4 * q + 4, :].bitcast(I32), y_scales[32 * q : 32 * q + 4, :].bitcast(I32))
